import numpy as np
import ml_dtypes


def mxq(x, axis, fmt="e4m3"):
    dtype, down = {"e4m3": (ml_dtypes.float8_e4m3fn, 7), "e5m2": (ml_dtypes.float8_e5m2, 14)}[fmt]
    v = np.moveaxis(np.asarray(x, np.float32).astype(ml_dtypes.bfloat16).astype(np.float64), axis, -1)
    blocks = v.reshape(v.shape[:-1] + (-1, 32))
    amax = np.abs(blocks).max(-1, keepdims=True)
    byte = np.maximum(np.where(amax > 0, np.frexp(amax)[1] - 1 + 127, 0) - down, 1)
    scale = np.exp2(byte - 127.0)
    codes = (blocks / scale).astype(np.float32).astype(dtype).astype(np.float64)
    return np.moveaxis((codes * scale).reshape(v.shape), -1, axis)


WIDE = False


def mx_kscale(k):
    if not WIDE:
        return np.ones(k)
    levels = np.array([10, -10, 5, -5, 0])
    if k % 512:
        return np.exp2(np.random.permutation(np.resize(levels, k // 32))).repeat(32)
    a = np.empty((k // 512, 16))
    for p in range(k // 512):
        a[p, :8] = np.random.permutation(np.resize(levels, 8))
        for g in range(8):
            far = levels[np.abs(levels - a[p, g]) >= 10]
            a[p, g + 8] = far[np.random.randint(len(far))]
    return np.exp2(a.ravel()).repeat(32)


def f64(x):
    return np.asarray(x).astype(np.float64)


def striped(idx):
    return np.tile(idx.reshape(-1, 16).T, (8, 1)).astype(np.uint16)


def unstriped(offs):
    return offs[:16].T.reshape(-1).astype(np.int64)


E2M1 = np.array([0.0, 0.5, 1.0, 1.5, 2.0, 3.0, 4.0, 6.0, -0.0, -0.5, -1.0, -1.5, -2.0, -3.0, -4.0, -6.0])


def pack_weight(w, fmt):
    k, n = w.shape
    w = f64(np.asarray(w, np.float32).astype(ml_dtypes.bfloat16)).reshape(k // 32, 32, n)
    amax = np.abs(w).max(1)
    if fmt == "e4m3":
        byte = np.frexp(amax)[1] - 1 + 127 - 7
    else:
        mant, ex = np.frexp(amax / 6.0)
        byte = np.where(mant > 0.5, ex, ex - 1) + 127
    byte = np.clip(np.where(amax > 0, byte, 1), 1, 254)
    scaled = (w * np.exp2(127.0 - byte)[:, None, :]).reshape(k, n).astype(np.float32)
    by_word = np.ascontiguousarray(scaled.reshape(k // 512, 128, 4, n).transpose(0, 1, 3, 2))
    if fmt == "e4m3":
        words = by_word.astype(ml_dtypes.float8_e4m3fn).view(np.uint8)
    else:
        c = by_word.astype(ml_dtypes.float4_e2m1fn).view(np.uint8) & 0xF
        words = (c[..., 0::2] | (c[..., 1::2] << 4)).reshape(k // 512, 128, 2 * n)
    return np.ascontiguousarray(words), np.ascontiguousarray(byte.astype(np.uint8).reshape(k // 512, 16, n))


def unpack_weight(words, scales, fmt):
    g, _, n = scales.shape
    words = np.ascontiguousarray(words).reshape(g, 128, n, -1)
    if fmt == "e4m3":
        vals = words.view(ml_dtypes.float8_e4m3fn).astype(np.float64)
    else:
        nib = np.empty((g, 128, n, 4), np.uint8)
        nib[..., 0::2] = words & 0xF
        nib[..., 1::2] = words >> 4
        vals = E2M1[nib]
    vals = vals * np.repeat(np.exp2(scales.astype(np.float64) - 127.0), 8, axis=1)[..., None]
    return vals.transpose(0, 1, 3, 2).reshape(g * 512, n)


def gelu(v):
    return 0.5 * v * (1.0 + np.tanh(np.sqrt(2.0 / np.pi) * (v + 0.044715 * v**3)))


K, T, S, H, T2, P = 1536, 2048, 1024, 512, 2048, 1024

def setup_inputs():
    n = np.random.standard_normal
    s = mx_kscale(K)[:, None]
    u = mx_kscale(H)[:, None]
    tab_words, tab_scales = pack_weight(n((K, T)) * s, "e4m3")
    w4_words, w4_scales = pack_weight(n((H, H)) / np.sqrt(H) / u * u.T, "e2m1")
    return {
        "tab_words": tab_words,
        "tab_scales": tab_scales,
        "offs": striped(np.random.permutation(T)[:S]),
        "w1": (n((K, H)) / np.sqrt(K) / s * u.T).astype(np.float32),
        "sv": (np.random.uniform(0.8, 2.0, H) / u[:, 0]).astype(np.float32),
        "page0": (n((H, T2)) * u).astype(np.float32),
        "wgs": np.exp(0.3 * n((128, S))).astype(np.float32),
        "offs2": striped(np.random.permutation(T2)[:S]),
        "offs3": striped(np.random.permutation(T2)[:P]),
        "temp": (0.8 * n((H, P)) * u).astype(np.float32),
        "w4_words": w4_words,
        "w4_scales": w4_scales,
        "gain": np.exp(0.4 * n(H)).astype(np.float32),
        "wgo": np.exp(0.3 * n((128, P))).astype(np.float32),
        "offs4": striped(np.random.permutation(T2)[:P]),
    }

def reference(tab_words, tab_scales, offs, w1, sv, page0, wgs, offs2, offs3, temp, w4_words, w4_scales, gain, wgo, offs4):
    v = unpack_weight(tab_words, tab_scales, "e4m3")[:, unstriped(offs)]
    a = mxq(f64(w1), 0, "e4m3").T @ v
    h = a * np.tanh(f64(sv)[:, None] * a)
    page = f64(page0).copy()
    page[:, unstriped(offs2)] = np.tile(f64(wgs), (H // 128, 1)) * h
    x = page[:, unstriped(offs3)] + f64(temp)
    w4 = unpack_weight(w4_words, w4_scales, "e2m1")
    y = f64(gain)[:, None] * (w4.T @ mxq(x, 0, "e4m3"))
    page[:, unstriped(offs4)] = np.tile(f64(wgo), (H // 128, 1)) * y
    return page

@@ -1,0 +1,209 @@
+from contextlib import ExitStack
+
+import concourse.mybir as mybir
+
+K, T, S, H, T2, PJ = 1536, 2048, 1024, 512, 2048, 1024
+FLOPS = 2 * K * H * S + 2 * H * H * PJ
+
+F32 = mybir.dt.float32
+BF16 = mybir.dt.bfloat16
+I32 = mybir.dt.int32
+U32 = mybir.dt.uint32
+U16 = mybir.dt.uint16
+U8 = mybir.dt.uint8
+FP8X4 = mybir.dt.float8_e4m3fn_x4
+FP4X4 = mybir.dt.float4_e2m1fn_x4
+MULT = mybir.AluOpType.mult
+ADD = mybir.AluOpType.add
+ACT = mybir.ActivationFunctionType
+
+P = 128
+PACK = 4
+PASSES = K // (P * PACK)
+QUADS = 4
+QUAD = P // QUADS
+BANK = 512
+STRIPE = 16
+CHUNKS = [(0, 256), (256, 512), (512, 1024)]
+
+
+def tile_list_rack_imbalance_page_kernel(
+    tc, tab_words, tab_scales, offs, w1, sv, page0, wgs, offs2, offs3, temp, w4_words, w4_scales, gain, wgo, offs4, out
+):
+    nc = tc.nc
+    with ExitStack() as ctx:
+        keep = ctx.enter_context(tc.tile_pool(name="keep", bufs=1))
+        ring = ctx.enter_context(tc.tile_pool(name="ring", bufs=1))
+        psum = ctx.enter_context(tc.psum_pool(name="psum", bufs=8))
+
+        def held(name, shape, dtype):
+            return keep.tile(shape, dtype, name=name, align_bytes=64)
+
+        def entries(list_tile, lo, hi):
+            return list_tile[:, lo // STRIPE : hi // STRIPE]
+
+        list1 = keep.tile([P, S // STRIPE], U16, name="list1")
+        list2 = keep.tile([P, S // STRIPE], U16, name="list2")
+        list3 = keep.tile([P, PJ // STRIPE], U16, name="list3")
+        list4 = keep.tile([P, PJ // STRIPE], U16, name="list4")
+
+        tab_w = [held(f"tab_w{a}", [P, T], U32) for a in range(PASSES)]
+        tab_s = held("tab_s", [P, T], U8)
+        w1_raw = [held(f"w1_raw{a}", [P, PACK, H], F32) for a in range(PASSES)]
+        pages = [held(f"page{t}", [P, T2], F32) for t in range(PACK)]
+        wgs_sb = [held(f"wgs{t}", [P, S], F32) for t in range(PACK)]
+        wgo_sb = held("wgo_sb", [P, PACK, PJ], F32)
+        temp_sb = held("temp_sb", [P, PACK, PJ], F32)
+        sv_sb = held("sv_sb", [P, PACK], F32)
+        gain_sb = held("gain_sb", [P, PACK], F32)
+        w4_raw = held("w4_raw", [P, 2 * H], U8)
+        w4s_raw = held("w4s_raw", [P, H], U8)
+
+        nc.vector.memset(tab_s[:].bitcast(I32), 0)
+        nc.gpsimd.memset(w4s_raw[:].bitcast(I32), 0)
+        nc.gpsimd.dma_start(out=w4_raw[:].bitcast(I32), in_=w4_words[0].bitcast(I32))
+        for q in range(QUADS):
+            nc.gpsimd.dma_start(
+                out=w4s_raw[QUAD * q : QUAD * q + 4, :].bitcast(I32),
+                in_=w4_scales[0, 4 * q : 4 * q + 4, :].bitcast(I32),
+            )
+        nc.gpsimd.dma_start(out=gain_sb[:], in_=gain.rearrange("(p t) -> p t", t=PACK))
+
+        page_rows = page0.rearrange("(p t) c -> t p c", t=PACK)
+        out_rows = out.rearrange("(p t) c -> t p c", t=PACK)
+        wgs_rows = wgs.rearrange("(p t) j -> t p j", t=PACK)
+        wgo_rows = wgo.rearrange("(p t) j -> p t j", t=PACK)
+
+        nc.sync.dma_start(list1[:], offs)
+        nc.sync.dma_start(list2[:], offs2)
+        nc.sync.dma_start(out=sv_sb[:], in_=sv.rearrange("(p t) -> p t", t=PACK))
+        for a in range(PASSES):
+            rows = w1[a * P * PACK : (a + 1) * P * PACK, :]
+            nc.sync.dma_start(out=w1_raw[a][:], in_=rows.rearrange("(p i) c -> p i c", i=PACK))
+            nc.sync.dma_start(
+                out=tab_w[a][:].bitcast(I32), in_=tab_words[a].rearrange("p n i -> p (n i)").bitcast(I32)
+            )
+            if a == 0:
+                for q in range(QUADS):
+                    nc.sync.dma_start(
+                        out=tab_s[QUAD * q : QUAD * q + 4 * PASSES, :].bitcast(I32),
+                        in_=tab_scales[:, 4 * q : 4 * q + 4, :].bitcast(I32),
+                    )
+        for t in range(PACK):
+            for q in range(QUADS):
+                nc.sync.dma_start(out=wgs_sb[t][QUAD * q : QUAD * (q + 1), :], in_=wgs_rows[t])
+            nc.sync.dma_start(out=pages[t][:], in_=page_rows[t])
+        nc.sync.dma_start(list3[:], offs3)
+        nc.sync.dma_start(out=temp_sb[:], in_=temp.rearrange("(p t) j -> p t j", t=PACK))
+        nc.sync.dma_start(list4[:], offs4)
+        for q in range(QUADS):
+            nc.sync.dma_start(out=wgo_sb[QUAD * q : QUAD * (q + 1), :, :], in_=wgo_rows)
+
+        v_s = held("v_s", [P, S], U8)
+        w1_q, w1_s, v_w = [], [], []
+        for a in range(PASSES):
+            w1_bf = ring.tile([P, PACK * H], BF16, name="w1_bf", bufs=2, align_bytes=64)
+            nc.scalar.copy(
+                out=w1_bf[:].rearrange("p (t m i) -> p m i t", t=PACK, i=PACK),
+                in_=w1_raw[a][:].rearrange("p i (m t) -> p m i t", t=PACK),
+            )
+            w1_q.append(held(f"w1_q{a}", [P, H], U32))
+            w1_s.append(held(f"w1_s{a}", [P, H], U8))
+            nc.vector.quantize_mx(out=w1_q[a][:].bitcast(FP8X4), scales=w1_s[a][:], in_=w1_bf[:])
+            v_w.append(held(f"v_w{a}", [P, S], U32))
+            step = BANK if a == PASSES - 1 else S
+            for lo in range(0, S, step):
+                nc.vector.tensor_copy(v_w[a][:, lo : lo + step], tab_w[a][:].indirect(entries(list1, lo, lo + step)))
+            if a == 0:
+                nc.vector.tensor_copy(v_s[:], tab_s[:].indirect(list1[:]))
+
+        w4_q = held("w4_q", [P, 2 * H], U8)
+        w4_s = held("w4_s", [P, H], U8)
+        nc.gpsimd.tensor_copy(
+            out=w4_q[:].rearrange("p (t m b) -> p t m b", t=PACK, b=2),
+            in_=w4_raw[:].rearrange("p (m t b) -> p t m b", t=PACK, b=2),
+        )
+        nc.gpsimd.tensor_copy(
+            out=w4_s[:].rearrange("p (t m) -> p t m", t=PACK),
+            in_=w4s_raw[:].rearrange("p (m t) -> p t m", t=PACK),
+        )
+
+        for t in range(PACK):
+            cols = slice(t * P, (t + 1) * P)
+            h = ring.tile([P, S], F32, name="vals", bufs=PACK)
+            for lo in range(0, S, BANK):
+                js = slice(lo, lo + BANK)
+                acc = psum.tile([P, BANK], F32, name="acc")
+                for a in range(PASSES):
+                    nc.tensor.matmul_mx(
+                        out=acc[:],
+                        lhsT=w1_q[a][:, cols].bitcast(FP8X4),
+                        lhsT_scale=w1_s[a][:, cols],
+                        rhs=v_w[a][:, js].bitcast(FP8X4),
+                        rhs_scale=v_s[4 * a : P, js],
+                        start=(a == 0),
+                        stop=(a == PASSES - 1),
+                    )
+                th = ring.tile([P, BANK], F32, name="th", bufs=3)
+                nc.scalar.activation(th[:], acc[:], ACT.Tanh, scale=sv_sb[:, t : t + 1])
+                nc.vector.tensor_tensor(h[:, js], acc[:], th[:], MULT)
+                if t == 0:
+                    nc.vector.tensor_tensor(
+                        pages[t][:].indirect(entries(list2, lo, lo + BANK)), h[:, js], wgs_sb[t][:, js], MULT
+                    )
+            if t > 0:
+                nc.vector.tensor_tensor(pages[t][:].indirect(list2[:]), h[:], wgs_sb[t][:], MULT)
+
+        x = held("x", [P, PACK, PJ], F32)
+        for lo, hi in CHUNKS:
+            for t in range(PACK):
+                nc.vector.tensor_tensor(
+                    x[:, t, lo:hi], pages[t][:].indirect(entries(list3, lo, hi)), temp_sb[:, t, lo:hi], ADD
+                )
+        ys = [ring.tile([P, PJ], F32, name="vals", bufs=PACK) for t in range(PACK)]
+        accs = {}
+
+        def product(lo, hi):
+            n = hi - lo
+            x_bf = held(f"x_bf{lo}", [P, PACK * n], BF16)
+            nc.scalar.copy(
+                out=x_bf[:].rearrange("p (c i t) -> p c t i", i=4, t=PACK),
+                in_=x[:, :, lo:hi].rearrange("p t (c i) -> p c t i", i=4),
+            )
+            x_q = held(f"x_q{lo}", [P, n], U32)
+            x_s = held(f"x_s{lo}", [P, n], U8)
+            nc.vector.quantize_mx(out=x_q[:].bitcast(FP8X4), scales=x_s[:], in_=x_bf[:])
+            for t in range(PACK):
+                acc = psum.tile([P, BANK], F32, name="acc")
+                nc.tensor.matmul_mx(
+                    out=acc[:, 0:n],
+                    lhsT=w4_q[:, 2 * t * P : 2 * (t + 1) * P].bitcast(FP4X4),
+                    lhsT_scale=w4_s[:, t * P : (t + 1) * P],
+                    rhs=x_q[:].bitcast(FP8X4),
+                    rhs_scale=x_s[:],
+                    start=True,
+                    stop=True,
+                )
+                accs[lo, t] = acc
+
+        def leave_psum(lo, hi):
+            for t in range(PACK):
+                nc.scalar.activation(ys[t][:, lo:hi], accs[lo, t][:, 0 : hi - lo], ACT.Copy, scale=gain_sb[:, t : t + 1])
+
+        def write(lo, hi):
+            for t in range(PACK):
+                nc.vector.tensor_tensor(
+                    pages[t][:].indirect(entries(list4, lo, hi)), ys[t][:, lo:hi], wgo_sb[:, t, lo:hi], MULT
+                )
+                if hi == PJ:
+                    nc.sync.dma_start(out=out_rows[t], in_=pages[t][:])
+
+        product(*CHUNKS[0])
+        leave_psum(*CHUNKS[0])
+        product(*CHUNKS[1])
+        product(*CHUNKS[2])
+        write(*CHUNKS[0])
+        leave_psum(*CHUNKS[1])
+        write(*CHUNKS[1])
+        leave_psum(*CHUNKS[2])
+        write(*CHUNKS[2])

@@ -24,6 +24,7 @@ QUADS = 4
 QUAD = P // QUADS
 BANK = 512
 STRIPE = 16
+LEAD = 256
 CHUNKS = [(0, 256), (256, 512), (512, 1024)]
 
 
@@ -51,7 +52,7 @@ def tile_list_rack_imbalance_page_kernel(
         tab_s = held("tab_s", [P, T], U8)
         w1_raw = [held(f"w1_raw{a}", [P, PACK, H], F32) for a in range(PASSES)]
         pages = [held(f"page{t}", [P, T2], F32) for t in range(PACK)]
-        wgs_sb = [held(f"wgs{t}", [P, S], F32) for t in range(PACK)]
+        wgs_sb = held("wgs_sb", [P, PACK * S], F32)
         wgo_sb = held("wgo_sb", [P, PACK, PJ], F32)
         temp_sb = held("temp_sb", [P, PACK, PJ], F32)
         sv_sb = held("sv_sb", [P, PACK], F32)
@@ -59,7 +60,7 @@ def tile_list_rack_imbalance_page_kernel(
         w4_raw = held("w4_raw", [P, 2 * H], U8)
         w4s_raw = held("w4s_raw", [P, H], U8)
 
-        nc.vector.memset(tab_s[:].bitcast(I32), 0)
+        nc.gpsimd.memset(tab_s[:].bitcast(I32), 0)
         nc.gpsimd.memset(w4s_raw[:].bitcast(I32), 0)
         nc.gpsimd.dma_start(out=w4_raw[:].bitcast(I32), in_=w4_words[0].bitcast(I32))
         for q in range(QUADS):
@@ -67,39 +68,54 @@ def tile_list_rack_imbalance_page_kernel(
                 out=w4s_raw[QUAD * q : QUAD * q + 4, :].bitcast(I32),
                 in_=w4_scales[0, 4 * q : 4 * q + 4, :].bitcast(I32),
             )
-        nc.gpsimd.dma_start(out=gain_sb[:], in_=gain.rearrange("(p t) -> p t", t=PACK))
 
         page_rows = page0.rearrange("(p t) c -> t p c", t=PACK)
         out_rows = out.rearrange("(p t) c -> t p c", t=PACK)
-        wgs_rows = wgs.rearrange("(p t) j -> t p j", t=PACK)
+        wgs_rows = wgs.rearrange("(p t) j -> p (t j)", t=PACK)
         wgo_rows = wgo.rearrange("(p t) j -> p t j", t=PACK)
 
-        nc.sync.dma_start(list1[:], offs)
-        nc.sync.dma_start(list2[:], offs2)
-        nc.sync.dma_start(out=sv_sb[:], in_=sv.rearrange("(p t) -> p t", t=PACK))
-        for a in range(PASSES):
+        def load_w1(a):
             rows = w1[a * P * PACK : (a + 1) * P * PACK, :]
             nc.sync.dma_start(out=w1_raw[a][:], in_=rows.rearrange("(p i) c -> p i c", i=PACK))
+
+        def load_table(a):
             nc.sync.dma_start(
                 out=tab_w[a][:].bitcast(I32), in_=tab_words[a].rearrange("p n i -> p (n i)").bitcast(I32)
             )
-            if a == 0:
-                for q in range(QUADS):
-                    nc.sync.dma_start(
-                        out=tab_s[QUAD * q : QUAD * q + 4 * PASSES, :].bitcast(I32),
-                        in_=tab_scales[:, 4 * q : 4 * q + 4, :].bitcast(I32),
-                    )
-        for t in range(PACK):
-            for q in range(QUADS):
-                nc.sync.dma_start(out=wgs_sb[t][QUAD * q : QUAD * (q + 1), :], in_=wgs_rows[t])
-            nc.sync.dma_start(out=pages[t][:], in_=page_rows[t])
+
+        def load_wgs(lo, hi):
+            for q in (0, 2, 1, 3):
+                nc.sync.dma_start(out=wgs_sb[QUAD * q : QUAD * (q + 1), lo:hi], in_=wgs_rows[:, lo:hi])
+
+        nc.sync.dma_start(list1[:], offs)
+        nc.sync.dma_start(list2[:], offs2)
+        load_table(0)
+        load_w1(0)
+        nc.sync.dma_start(out=sv_sb[:], in_=sv.rearrange("(p t) -> p t", t=PACK))
+        nc.sync.dma_start(out=gain_sb[:], in_=gain.rearrange("(p t) -> p t", t=PACK))
+        load_w1(1)
+        for q in range(QUADS):
+            nc.scalar.dma_start(
+                out=tab_s[QUAD * q : QUAD * q + 4 * PASSES, :].bitcast(I32),
+                in_=tab_scales[:, 4 * q : 4 * q + 4, :].bitcast(I32),
+            )
+        load_table(1)
+        load_w1(2)
+        load_table(2)
+        load_wgs(0, LEAD)
+        nc.sync.dma_start(out=pages[0][:], in_=page_rows[0])
+        load_wgs(LEAD, S)
+        load_wgs(S, 2 * S)
+        nc.sync.dma_start(out=pages[1][:], in_=page_rows[1])
+        load_wgs(2 * S, PACK * S)
+        nc.sync.dma_start(out=pages[2][:], in_=page_rows[2])
+        nc.sync.dma_start(out=pages[3][:], in_=page_rows[3])
+        nc.sync.dma_start(list4[:], offs4)
+        for q in (0, 2, 1, 3):
+            nc.sync.dma_start(out=wgo_sb[QUAD * q : QUAD * (q + 1), :, :], in_=wgo_rows)
         nc.sync.dma_start(list3[:], offs3)
         nc.sync.dma_start(out=temp_sb[:], in_=temp.rearrange("(p t) j -> p t j", t=PACK))
-        nc.sync.dma_start(list4[:], offs4)
-        for q in range(QUADS):
-            nc.sync.dma_start(out=wgo_sb[QUAD * q : QUAD * (q + 1), :, :], in_=wgo_rows)
 
-        v_s = held("v_s", [P, S], U8)
         w1_q, w1_s, v_w = [], [], []
         for a in range(PASSES):
             w1_bf = ring.tile([P, PACK * H], BF16, name="w1_bf", bufs=2, align_bytes=64)
@@ -111,10 +127,10 @@ def tile_list_rack_imbalance_page_kernel(
             w1_s.append(held(f"w1_s{a}", [P, H], U8))
             nc.vector.quantize_mx(out=w1_q[a][:].bitcast(FP8X4), scales=w1_s[a][:], in_=w1_bf[:])
             v_w.append(held(f"v_w{a}", [P, S], U32))
-            step = BANK if a == PASSES - 1 else S
-            for lo in range(0, S, step):
-                nc.vector.tensor_copy(v_w[a][:, lo : lo + step], tab_w[a][:].indirect(entries(list1, lo, lo + step)))
+            for lo, hi in [(0, LEAD), (LEAD, S)] if a == PASSES - 1 else [(0, S)]:
+                nc.vector.tensor_copy(v_w[a][:, lo:hi], tab_w[a][:].indirect(entries(list1, lo, hi)))
             if a == 0:
+                v_s = held("tab_w0", [P, S], U8)
                 nc.vector.tensor_copy(v_s[:], tab_s[:].indirect(list1[:]))
 
         w4_q = held("w4_q", [P, 2 * H], U8)
@@ -131,47 +147,55 @@ def tile_list_rack_imbalance_page_kernel(
         for t in range(PACK):
             cols = slice(t * P, (t + 1) * P)
             h = ring.tile([P, S], F32, name="vals", bufs=PACK)
-            for lo in range(0, S, BANK):
-                js = slice(lo, lo + BANK)
+            order = list(range(PASSES)) if t == 0 else list(reversed(range(PASSES)))
+            sums = [(0, LEAD), (LEAD, BANK), (BANK, S)] if t == 0 else [(0, BANK), (BANK, S)]
+            writes = {LEAD: 0, S: LEAD} if t == 0 else {S: 0}
+            for lo, hi in sums:
+                n = hi - lo
                 acc = psum.tile([P, BANK], F32, name="acc")
-                for a in range(PASSES):
+                for a in order:
                     nc.tensor.matmul_mx(
-                        out=acc[:],
+                        out=acc[:, 0:n],
                         lhsT=w1_q[a][:, cols].bitcast(FP8X4),
                         lhsT_scale=w1_s[a][:, cols],
-                        rhs=v_w[a][:, js].bitcast(FP8X4),
-                        rhs_scale=v_s[4 * a : P, js],
-                        start=(a == 0),
-                        stop=(a == PASSES - 1),
+                        rhs=v_w[a][:, lo:hi].bitcast(FP8X4),
+                        rhs_scale=v_s[4 * a : P, lo:hi],
+                        start=(a == order[0]),
+                        stop=(a == order[-1]),
                     )
                 th = ring.tile([P, BANK], F32, name="th", bufs=3)
-                nc.scalar.activation(th[:], acc[:], ACT.Tanh, scale=sv_sb[:, t : t + 1])
-                nc.vector.tensor_tensor(h[:, js], acc[:], th[:], MULT)
-                if t == 0:
+                nc.scalar.activation(th[:, 0:n], acc[:, 0:n], ACT.Tanh, scale=sv_sb[:, t : t + 1])
+                nc.vector.tensor_tensor(h[:, lo:hi], acc[:, 0:n], th[:, 0:n], MULT)
+                if hi in writes:
+                    first = writes[hi]
                     nc.vector.tensor_tensor(
-                        pages[t][:].indirect(entries(list2, lo, lo + BANK)), h[:, js], wgs_sb[t][:, js], MULT
+                        pages[t][:].indirect(entries(list2, first, hi)),
+                        h[:, first:hi],
+                        wgs_sb[:, t * S + first : t * S + hi],
+                        MULT,
                     )
-            if t > 0:
-                nc.vector.tensor_tensor(pages[t][:].indirect(list2[:]), h[:], wgs_sb[t][:], MULT)
 
-        x = held("x", [P, PACK, PJ], F32)
-        for lo, hi in CHUNKS:
+        xs, x_bfs, accs, ys = {}, {}, {}, {}
+
+        def relay(shape, dtype):
+            return ring.tile(shape, dtype, name="relay", bufs=1, align_bytes=64)
+
+        def fetch(c, x):
+            lo, hi = CHUNKS[c]
+            xs[c] = x
             for t in range(PACK):
                 nc.vector.tensor_tensor(
-                    x[:, t, lo:hi], pages[t][:].indirect(entries(list3, lo, hi)), temp_sb[:, t, lo:hi], ADD
+                    x[:, t, :], pages[t][:].indirect(entries(list3, lo, hi)), temp_sb[:, t, lo:hi], ADD
                 )
-        ys = [ring.tile([P, PJ], F32, name="vals", bufs=PACK) for t in range(PACK)]
-        accs = {}
 
-        def product(lo, hi):
-            n = hi - lo
-            x_bf = held(f"x_bf{lo}", [P, PACK * n], BF16)
+        def product(c, x_bf):
+            n = CHUNKS[c][1] - CHUNKS[c][0]
             nc.scalar.copy(
                 out=x_bf[:].rearrange("p (c i t) -> p c t i", i=4, t=PACK),
-                in_=x[:, :, lo:hi].rearrange("p t (c i) -> p c t i", i=4),
+                in_=xs[c][:].rearrange("p t (c i) -> p c t i", i=4),
             )
-            x_q = held(f"x_q{lo}", [P, n], U32)
-            x_s = held(f"x_s{lo}", [P, n], U8)
+            x_q = held(f"x_q{c}", [P, n], U32)
+            x_s = held(f"x_s{c}", [P, n], U8)
             nc.vector.quantize_mx(out=x_q[:].bitcast(FP8X4), scales=x_s[:], in_=x_bf[:])
             for t in range(PACK):
                 acc = psum.tile([P, BANK], F32, name="acc")
@@ -184,26 +208,33 @@ def tile_list_rack_imbalance_page_kernel(
                     start=True,
                     stop=True,
                 )
-                accs[lo, t] = acc
+                accs[c, t] = acc
 
-        def leave_psum(lo, hi):
+        def leave_psum(c, y):
+            n = CHUNKS[c][1] - CHUNKS[c][0]
+            ys[c] = y
             for t in range(PACK):
-                nc.scalar.activation(ys[t][:, lo:hi], accs[lo, t][:, 0 : hi - lo], ACT.Copy, scale=gain_sb[:, t : t + 1])
+                nc.scalar.activation(y[:, t, :], accs[c, t][:, 0:n], ACT.Copy, scale=gain_sb[:, t : t + 1])
 
-        def write(lo, hi):
+        def write(c):
+            lo, hi = CHUNKS[c]
             for t in range(PACK):
                 nc.vector.tensor_tensor(
-                    pages[t][:].indirect(entries(list4, lo, hi)), ys[t][:, lo:hi], wgo_sb[:, t, lo:hi], MULT
+                    pages[t][:].indirect(entries(list4, lo, hi)), ys[c][:, t, :], wgo_sb[:, t, lo:hi], MULT
                 )
                 if hi == PJ:
                     nc.sync.dma_start(out=out_rows[t], in_=pages[t][:])
 
-        product(*CHUNKS[0])
-        leave_psum(*CHUNKS[0])
-        product(*CHUNKS[1])
-        product(*CHUNKS[2])
-        write(*CHUNKS[0])
-        leave_psum(*CHUNKS[1])
-        write(*CHUNKS[1])
-        leave_psum(*CHUNKS[2])
-        write(*CHUNKS[2])
+        widths = [hi - lo for lo, hi in CHUNKS]
+        fetch(0, held("x0", [P, PACK, widths[0]], F32))
+        fetch(1, held("x1", [P, PACK, widths[1]], F32))
+        product(0, relay([P, PACK * widths[0]], BF16))
+        fetch(2, relay([P, PACK, widths[2]], F32))
+        leave_psum(0, held("y0", [P, PACK, widths[0]], F32))
+        product(1, held("x_bf1", [P, PACK * widths[1]], BF16))
+        product(2, held("x_bf2", [P, PACK * widths[2]], BF16))
+        write(0)
+        leave_psum(1, relay([P, PACK, widths[1]], F32))
+        write(1)
+        leave_psum(2, held("y2", [P, PACK, widths[2]], F32))
+        write(2)

@@ -99,8 +99,8 @@ def tile_list_rack_imbalance_page_kernel(
                 out=tab_s[QUAD * q : QUAD * q + 4 * PASSES, :].bitcast(I32),
                 in_=tab_scales[:, 4 * q : 4 * q + 4, :].bitcast(I32),
             )
-        load_table(1)
         load_w1(2)
+        load_table(1)
         load_table(2)
         load_wgs(0, LEAD)
         nc.sync.dma_start(out=pages[0][:], in_=page_rows[0])
@@ -144,36 +144,45 @@ def tile_list_rack_imbalance_page_kernel(
             in_=w4s_raw[:].rearrange("p (m t) -> p t m", t=PACK),
         )
 
-        for t in range(PACK):
+        def first_product(t, lo, hi):
             cols = slice(t * P, (t + 1) * P)
-            h = ring.tile([P, S], F32, name="vals", bufs=PACK)
-            order = list(range(PASSES)) if t == 0 else list(reversed(range(PASSES)))
-            sums = [(0, LEAD), (LEAD, BANK), (BANK, S)] if t == 0 else [(0, BANK), (BANK, S)]
-            writes = {LEAD: 0, S: LEAD} if t == 0 else {S: 0}
-            for lo, hi in sums:
-                n = hi - lo
-                acc = psum.tile([P, BANK], F32, name="acc")
-                for a in order:
-                    nc.tensor.matmul_mx(
-                        out=acc[:, 0:n],
-                        lhsT=w1_q[a][:, cols].bitcast(FP8X4),
-                        lhsT_scale=w1_s[a][:, cols],
-                        rhs=v_w[a][:, lo:hi].bitcast(FP8X4),
-                        rhs_scale=v_s[4 * a : P, lo:hi],
-                        start=(a == order[0]),
-                        stop=(a == order[-1]),
-                    )
-                th = ring.tile([P, BANK], F32, name="th", bufs=3)
-                nc.scalar.activation(th[:, 0:n], acc[:, 0:n], ACT.Tanh, scale=sv_sb[:, t : t + 1])
-                nc.vector.tensor_tensor(h[:, lo:hi], acc[:, 0:n], th[:, 0:n], MULT)
-                if hi in writes:
-                    first = writes[hi]
-                    nc.vector.tensor_tensor(
-                        pages[t][:].indirect(entries(list2, first, hi)),
-                        h[:, first:hi],
-                        wgs_sb[:, t * S + first : t * S + hi],
-                        MULT,
-                    )
+            order = list(range(PASSES)) if t < 2 else list(reversed(range(PASSES)))
+            acc = psum.tile([P, BANK], F32, name="acc")
+            for a in order:
+                nc.tensor.matmul_mx(
+                    out=acc[:, 0 : hi - lo],
+                    lhsT=w1_q[a][:, cols].bitcast(FP8X4),
+                    lhsT_scale=w1_s[a][:, cols],
+                    rhs=v_w[a][:, lo:hi].bitcast(FP8X4),
+                    rhs_scale=v_s[4 * a : P, lo:hi],
+                    start=(a == order[0]),
+                    stop=(a == order[-1]),
+                )
+            return acc[:, 0 : hi - lo]
+
+        th = ring.tile([P, S], F32, name="th", bufs=2)
+        h = ring.tile([P, S], F32, name="part", bufs=1)
+        for lo, hi in [(0, LEAD), (LEAD, BANK), (BANK, S)]:
+            acc = first_product(0, lo, hi)
+            nc.scalar.activation(th[:, lo:hi], acc, ACT.Tanh, scale=sv_sb[:, 0:1])
+            nc.vector.tensor_tensor(h[:, lo:hi], acc, th[:, lo:hi], MULT)
+            if hi == LEAD:
+                nc.vector.tensor_tensor(pages[0][:].indirect(entries(list2, lo, hi)), h[:, lo:hi], wgs_sb[:, lo:hi], MULT)
+        vals = ring.tile([P, S], F32, name="vals", bufs=2)
+        nc.vector.tensor_tensor(vals[:, LEAD:S], h[:, LEAD:S], wgs_sb[:, LEAD:S], MULT)
+        nc.vector.tensor_copy(pages[0][:].indirect(entries(list2, LEAD, S)), vals[:, LEAD:S])
+        for t in range(1, PACK):
+            th = ring.tile([P, S], F32, name="th", bufs=2)
+            a_sb = ring.tile([P, S], F32, name="a_sb", bufs=2)
+            for lo in range(0, S, BANK):
+                acc = first_product(t, lo, lo + BANK)
+                nc.scalar.activation(th[:, lo : lo + BANK], acc, ACT.Tanh, scale=sv_sb[:, t : t + 1])
+                nc.scalar.copy(a_sb[:, lo : lo + BANK], acc)
+            h = ring.tile([P, S], F32, name="part", bufs=1)
+            nc.gpsimd.tensor_tensor(h[:], a_sb[:], th[:], MULT)
+            vals = ring.tile([P, S], F32, name="vals", bufs=2)
+            nc.gpsimd.tensor_tensor(vals[:], h[:], wgs_sb[:, t * S : (t + 1) * S], MULT)
+            nc.vector.tensor_copy(pages[t][:].indirect(list2[:]), vals[:])
 
         xs, x_bfs, accs, ys = {}, {}, {}, {}
 

@@ -24,7 +24,6 @@ QUADS = 4
 QUAD = P // QUADS
 BANK = 512
 STRIPE = 16
-LEAD = 256
 CHUNKS = [(0, 256), (256, 512), (512, 1024)]
 
 
@@ -61,6 +60,11 @@ def tile_list_rack_imbalance_page_kernel(
         w4s_raw = held("w4s_raw", [P, H], U8)
 
         nc.gpsimd.memset(tab_s[:].bitcast(I32), 0)
+        for q in range(QUADS):
+            nc.gpsimd.dma_start(
+                out=tab_s[QUAD * q : QUAD * q + 4 * PASSES, :].bitcast(I32),
+                in_=tab_scales[:, 4 * q : 4 * q + 4, :].bitcast(I32),
+            )
         nc.gpsimd.memset(w4s_raw[:].bitcast(I32), 0)
         nc.gpsimd.dma_start(out=w4_raw[:].bitcast(I32), in_=w4_words[0].bitcast(I32))
         for q in range(QUADS):
@@ -87,34 +91,33 @@ def tile_list_rack_imbalance_page_kernel(
             for q in (0, 2, 1, 3):
                 nc.sync.dma_start(out=wgs_sb[QUAD * q : QUAD * (q + 1), lo:hi], in_=wgs_rows[:, lo:hi])
 
+        def load_wgo(lo, hi):
+            for q in (0, 2, 1, 3):
+                nc.sync.dma_start(out=wgo_sb[QUAD * q : QUAD * (q + 1), :, lo:hi], in_=wgo_rows[:, :, lo:hi])
+
+        def load_page(t):
+            nc.sync.dma_start(out=pages[t][:], in_=page_rows[t])
+
+        load_table(0)
         nc.sync.dma_start(list1[:], offs)
         nc.sync.dma_start(list2[:], offs2)
-        load_table(0)
-        load_w1(0)
         nc.sync.dma_start(out=sv_sb[:], in_=sv.rearrange("(p t) -> p t", t=PACK))
         nc.sync.dma_start(out=gain_sb[:], in_=gain.rearrange("(p t) -> p t", t=PACK))
-        load_w1(1)
-        for q in range(QUADS):
-            nc.scalar.dma_start(
-                out=tab_s[QUAD * q : QUAD * q + 4 * PASSES, :].bitcast(I32),
-                in_=tab_scales[:, 4 * q : 4 * q + 4, :].bitcast(I32),
-            )
-        load_w1(2)
+        for a in range(PASSES):
+            load_w1(a)
         load_table(1)
         load_table(2)
-        load_wgs(0, LEAD)
-        nc.sync.dma_start(out=pages[0][:], in_=page_rows[0])
-        load_wgs(LEAD, S)
-        load_wgs(S, 2 * S)
-        nc.sync.dma_start(out=pages[1][:], in_=page_rows[1])
-        load_wgs(2 * S, PACK * S)
-        nc.sync.dma_start(out=pages[2][:], in_=page_rows[2])
-        nc.sync.dma_start(out=pages[3][:], in_=page_rows[3])
-        nc.sync.dma_start(list4[:], offs4)
-        for q in (0, 2, 1, 3):
-            nc.sync.dma_start(out=wgo_sb[QUAD * q : QUAD * (q + 1), :, :], in_=wgo_rows)
+        load_wgs(0, BANK)
+        load_page(0)
+        load_wgs(BANK, S)
+        for t in range(1, PACK):
+            load_wgs(t * S, (t + 1) * S)
+            load_page(t)
         nc.sync.dma_start(list3[:], offs3)
+        nc.sync.dma_start(list4[:], offs4)
+        load_wgo(*CHUNKS[0])
         nc.sync.dma_start(out=temp_sb[:], in_=temp.rearrange("(p t) j -> p t j", t=PACK))
+        load_wgo(CHUNKS[0][1], PJ)
 
         w1_q, w1_s, v_w = [], [], []
         for a in range(PASSES):
@@ -127,7 +130,7 @@ def tile_list_rack_imbalance_page_kernel(
             w1_s.append(held(f"w1_s{a}", [P, H], U8))
             nc.vector.quantize_mx(out=w1_q[a][:].bitcast(FP8X4), scales=w1_s[a][:], in_=w1_bf[:])
             v_w.append(held(f"v_w{a}", [P, S], U32))
-            for lo, hi in [(0, LEAD), (LEAD, S)] if a == PASSES - 1 else [(0, S)]:
+            for lo, hi in [(0, BANK), (BANK, S)] if a == PASSES - 1 else [(0, S)]:
                 nc.vector.tensor_copy(v_w[a][:, lo:hi], tab_w[a][:].indirect(entries(list1, lo, hi)))
             if a == 0:
                 v_s = held("tab_w0", [P, S], U8)
@@ -160,29 +163,29 @@ def tile_list_rack_imbalance_page_kernel(
                 )
             return acc[:, 0 : hi - lo]
 
-        th = ring.tile([P, S], F32, name="th", bufs=2)
-        h = ring.tile([P, S], F32, name="part", bufs=1)
-        for lo, hi in [(0, LEAD), (LEAD, BANK), (BANK, S)]:
-            acc = first_product(0, lo, hi)
-            nc.scalar.activation(th[:, lo:hi], acc, ACT.Tanh, scale=sv_sb[:, 0:1])
-            nc.vector.tensor_tensor(h[:, lo:hi], acc, th[:, lo:hi], MULT)
-            if hi == LEAD:
-                nc.vector.tensor_tensor(pages[0][:].indirect(entries(list2, lo, hi)), h[:, lo:hi], wgs_sb[:, lo:hi], MULT)
-        vals = ring.tile([P, S], F32, name="vals", bufs=2)
-        nc.vector.tensor_tensor(vals[:, LEAD:S], h[:, LEAD:S], wgs_sb[:, LEAD:S], MULT)
-        nc.vector.tensor_copy(pages[0][:].indirect(entries(list2, LEAD, S)), vals[:, LEAD:S])
-        for t in range(1, PACK):
+        def soft_values(t, lo, hi, vals):
             th = ring.tile([P, S], F32, name="th", bufs=2)
-            a_sb = ring.tile([P, S], F32, name="a_sb", bufs=2)
-            for lo in range(0, S, BANK):
-                acc = first_product(t, lo, lo + BANK)
-                nc.scalar.activation(th[:, lo : lo + BANK], acc, ACT.Tanh, scale=sv_sb[:, t : t + 1])
-                nc.scalar.copy(a_sb[:, lo : lo + BANK], acc)
-            h = ring.tile([P, S], F32, name="part", bufs=1)
-            nc.gpsimd.tensor_tensor(h[:], a_sb[:], th[:], MULT)
+            h = ring.tile([P, S], F32, name="h", bufs=1)
+            lead = t == 0 and lo == 0
+            a_sb = None if lead else ring.tile([P, S], F32, name="a_sb", bufs=2)
+            for b in range(lo, hi, BANK):
+                js = slice(b, b + BANK)
+                acc = first_product(t, b, b + BANK)
+                nc.scalar.activation(th[:, js], acc, ACT.Tanh, scale=sv_sb[:, t : t + 1])
+                if lead:
+                    nc.vector.tensor_tensor(h[:, js], acc, th[:, js], MULT)
+                else:
+                    nc.scalar.copy(a_sb[:, js], acc)
+            if not lead:
+                nc.gpsimd.tensor_tensor(h[:, lo:hi], a_sb[:, lo:hi], th[:, lo:hi], MULT)
+            engine = nc.vector if lead else nc.gpsimd
+            engine.tensor_tensor(vals[:, lo:hi], h[:, lo:hi], wgs_sb[:, t * S + lo : t * S + hi], MULT)
+
+        for t in range(PACK):
             vals = ring.tile([P, S], F32, name="vals", bufs=2)
-            nc.gpsimd.tensor_tensor(vals[:], h[:], wgs_sb[:, t * S : (t + 1) * S], MULT)
-            nc.vector.tensor_copy(pages[t][:].indirect(list2[:]), vals[:])
+            for lo, hi in [(0, BANK), (BANK, S)] if t < 2 else [(0, S)]:
+                soft_values(t, lo, hi, vals)
+                nc.vector.tensor_copy(pages[t][:].indirect(entries(list2, lo, hi)), vals[:, lo:hi])
 
         xs, x_bfs, accs, ys = {}, {}, {}, {}
 

from contextlib import ExitStack

import concourse.mybir as mybir

K, T, S, H, T2, PJ = 1536, 2048, 1024, 512, 2048, 1024
FLOPS = 2 * K * H * S + 2 * H * H * PJ

F32 = mybir.dt.float32
BF16 = mybir.dt.bfloat16
I32 = mybir.dt.int32
U32 = mybir.dt.uint32
U16 = mybir.dt.uint16
U8 = mybir.dt.uint8
FP8X4 = mybir.dt.float8_e4m3fn_x4
FP4X4 = mybir.dt.float4_e2m1fn_x4
MULT = mybir.AluOpType.mult
ADD = mybir.AluOpType.add
ACT = mybir.ActivationFunctionType

P = 128
PACK = 4
PASSES = K // (P * PACK)
QUADS = 4
QUAD = P // QUADS
BANK = 512
STRIPE = 16
CHUNKS = [(0, 256), (256, 512), (512, 1024)]


def tile_list_rack_imbalance_page_kernel(
    tc, tab_words, tab_scales, offs, w1, sv, page0, wgs, offs2, offs3, temp, w4_words, w4_scales, gain, wgo, offs4, out
):
    nc = tc.nc
    with ExitStack() as ctx:
        keep = ctx.enter_context(tc.tile_pool(name="keep", bufs=1))
        ring = ctx.enter_context(tc.tile_pool(name="ring", bufs=1))
        psum = ctx.enter_context(tc.psum_pool(name="psum", bufs=8))

        def held(name, shape, dtype):
            return keep.tile(shape, dtype, name=name, align_bytes=64)

        def entries(list_tile, lo, hi):
            return list_tile[:, lo // STRIPE : hi // STRIPE]

        list1 = keep.tile([P, S // STRIPE], U16, name="list1")
        list2 = keep.tile([P, S // STRIPE], U16, name="list2")
        list3 = keep.tile([P, PJ // STRIPE], U16, name="list3")
        list4 = keep.tile([P, PJ // STRIPE], U16, name="list4")

        tab_w = [held(f"tab_w{a}", [P, T], U32) for a in range(PASSES)]
        tab_s = held("tab_s", [P, T], U8)
        w1_raw = [held(f"w1_raw{a}", [P, PACK, H], F32) for a in range(PASSES)]
        pages = [held(f"page{t}", [P, T2], F32) for t in range(PACK)]
        wgs_sb = held("wgs_sb", [P, PACK * S], F32)
        wgo_sb = held("wgo_sb", [P, PACK, PJ], F32)
        temp_sb = held("temp_sb", [P, PACK, PJ], F32)
        sv_sb = held("sv_sb", [P, PACK], F32)
        gain_sb = held("gain_sb", [P, PACK], F32)
        w4_raw = held("w4_raw", [P, 2 * H], U8)
        w4s_raw = held("w4s_raw", [P, H], U8)

        nc.gpsimd.memset(tab_s[:].bitcast(I32), 0)
        for q in range(QUADS):
            nc.gpsimd.dma_start(
                out=tab_s[QUAD * q : QUAD * q + 4 * PASSES, :].bitcast(I32),
                in_=tab_scales[:, 4 * q : 4 * q + 4, :].bitcast(I32),
            )
        nc.gpsimd.memset(w4s_raw[:].bitcast(I32), 0)
        nc.gpsimd.dma_start(out=w4_raw[:].bitcast(I32), in_=w4_words[0].bitcast(I32))
        for q in range(QUADS):
            nc.gpsimd.dma_start(
                out=w4s_raw[QUAD * q : QUAD * q + 4, :].bitcast(I32),
                in_=w4_scales[0, 4 * q : 4 * q + 4, :].bitcast(I32),
            )

        page_rows = page0.rearrange("(p t) c -> t p c", t=PACK)
        out_rows = out.rearrange("(p t) c -> t p c", t=PACK)
        wgs_rows = wgs.rearrange("(p t) j -> p (t j)", t=PACK)
        wgo_rows = wgo.rearrange("(p t) j -> p t j", t=PACK)

        def load_w1(a):
            rows = w1[a * P * PACK : (a + 1) * P * PACK, :]
            nc.sync.dma_start(out=w1_raw[a][:], in_=rows.rearrange("(p i) c -> p i c", i=PACK))

        def load_table(a):
            nc.sync.dma_start(
                out=tab_w[a][:].bitcast(I32), in_=tab_words[a].rearrange("p n i -> p (n i)").bitcast(I32)
            )

        def load_wgs(lo, hi):
            for q in (0, 2, 1, 3):
                nc.sync.dma_start(out=wgs_sb[QUAD * q : QUAD * (q + 1), lo:hi], in_=wgs_rows[:, lo:hi])

        def load_wgo(lo, hi):
            for q in (0, 2, 1, 3):
                nc.sync.dma_start(out=wgo_sb[QUAD * q : QUAD * (q + 1), :, lo:hi], in_=wgo_rows[:, :, lo:hi])

        def load_page(t):
            nc.sync.dma_start(out=pages[t][:], in_=page_rows[t])

        load_table(0)
        nc.sync.dma_start(list1[:], offs)
        nc.sync.dma_start(list2[:], offs2)
        nc.sync.dma_start(out=sv_sb[:], in_=sv.rearrange("(p t) -> p t", t=PACK))
        nc.sync.dma_start(out=gain_sb[:], in_=gain.rearrange("(p t) -> p t", t=PACK))
        for a in range(PASSES):
            load_w1(a)
        load_table(1)
        load_table(2)
        load_wgs(0, BANK)
        load_page(0)
        load_wgs(BANK, S)
        for t in range(1, PACK):
            load_wgs(t * S, (t + 1) * S)
            load_page(t)
        nc.sync.dma_start(list3[:], offs3)
        nc.sync.dma_start(list4[:], offs4)
        load_wgo(*CHUNKS[0])
        nc.sync.dma_start(out=temp_sb[:], in_=temp.rearrange("(p t) j -> p t j", t=PACK))
        load_wgo(CHUNKS[0][1], PJ)

        w1_q, w1_s, v_w = [], [], []
        for a in range(PASSES):
            w1_bf = ring.tile([P, PACK * H], BF16, name="w1_bf", bufs=2, align_bytes=64)
            nc.scalar.copy(
                out=w1_bf[:].rearrange("p (t m i) -> p m i t", t=PACK, i=PACK),
                in_=w1_raw[a][:].rearrange("p i (m t) -> p m i t", t=PACK),
            )
            w1_q.append(held(f"w1_q{a}", [P, H], U32))
            w1_s.append(held(f"w1_s{a}", [P, H], U8))
            nc.vector.quantize_mx(out=w1_q[a][:].bitcast(FP8X4), scales=w1_s[a][:], in_=w1_bf[:])
            v_w.append(held(f"v_w{a}", [P, S], U32))
            for lo, hi in [(0, BANK), (BANK, S)] if a == PASSES - 1 else [(0, S)]:
                nc.vector.tensor_copy(v_w[a][:, lo:hi], tab_w[a][:].indirect(entries(list1, lo, hi)))
            if a == 0:
                v_s = held("tab_w0", [P, S], U8)
                nc.vector.tensor_copy(v_s[:], tab_s[:].indirect(list1[:]))

        w4_q = held("w4_q", [P, 2 * H], U8)
        w4_s = held("w4_s", [P, H], U8)
        nc.gpsimd.tensor_copy(
            out=w4_q[:].rearrange("p (t m b) -> p t m b", t=PACK, b=2),
            in_=w4_raw[:].rearrange("p (m t b) -> p t m b", t=PACK, b=2),
        )
        nc.gpsimd.tensor_copy(
            out=w4_s[:].rearrange("p (t m) -> p t m", t=PACK),
            in_=w4s_raw[:].rearrange("p (m t) -> p t m", t=PACK),
        )

        def first_product(t, lo, hi):
            cols = slice(t * P, (t + 1) * P)
            order = list(range(PASSES)) if t < 2 else list(reversed(range(PASSES)))
            acc = psum.tile([P, BANK], F32, name="acc")
            for a in order:
                nc.tensor.matmul_mx(
                    out=acc[:, 0 : hi - lo],
                    lhsT=w1_q[a][:, cols].bitcast(FP8X4),
                    lhsT_scale=w1_s[a][:, cols],
                    rhs=v_w[a][:, lo:hi].bitcast(FP8X4),
                    rhs_scale=v_s[4 * a : P, lo:hi],
                    start=(a == order[0]),
                    stop=(a == order[-1]),
                )
            return acc[:, 0 : hi - lo]

        def soft_values(t, lo, hi, vals):
            th = ring.tile([P, S], F32, name="th", bufs=2)
            h = ring.tile([P, S], F32, name="h", bufs=1)
            lead = t == 0 and lo == 0
            a_sb = None if lead else ring.tile([P, S], F32, name="a_sb", bufs=2)
            for b in range(lo, hi, BANK):
                js = slice(b, b + BANK)
                acc = first_product(t, b, b + BANK)
                nc.scalar.activation(th[:, js], acc, ACT.Tanh, scale=sv_sb[:, t : t + 1])
                if lead:
                    nc.vector.tensor_tensor(h[:, js], acc, th[:, js], MULT)
                else:
                    nc.scalar.copy(a_sb[:, js], acc)
            if not lead:
                nc.gpsimd.tensor_tensor(h[:, lo:hi], a_sb[:, lo:hi], th[:, lo:hi], MULT)
            engine = nc.vector if lead else nc.gpsimd
            engine.tensor_tensor(vals[:, lo:hi], h[:, lo:hi], wgs_sb[:, t * S + lo : t * S + hi], MULT)

        for t in range(PACK):
            vals = ring.tile([P, S], F32, name="vals", bufs=2)
            for lo, hi in [(0, BANK), (BANK, S)] if t < 2 else [(0, S)]:
                soft_values(t, lo, hi, vals)
                nc.vector.tensor_copy(pages[t][:].indirect(entries(list2, lo, hi)), vals[:, lo:hi])

        xs, x_bfs, accs, ys = {}, {}, {}, {}

        def relay(shape, dtype):
            return ring.tile(shape, dtype, name="relay", bufs=1, align_bytes=64)

        def fetch(c, x):
            lo, hi = CHUNKS[c]
            xs[c] = x
            for t in range(PACK):
                nc.vector.tensor_tensor(
                    x[:, t, :], pages[t][:].indirect(entries(list3, lo, hi)), temp_sb[:, t, lo:hi], ADD
                )

        def product(c, x_bf):
            n = CHUNKS[c][1] - CHUNKS[c][0]
            nc.scalar.copy(
                out=x_bf[:].rearrange("p (c i t) -> p c t i", i=4, t=PACK),
                in_=xs[c][:].rearrange("p t (c i) -> p c t i", i=4),
            )
            x_q = held(f"x_q{c}", [P, n], U32)
            x_s = held(f"x_s{c}", [P, n], U8)
            nc.vector.quantize_mx(out=x_q[:].bitcast(FP8X4), scales=x_s[:], in_=x_bf[:])
            for t in range(PACK):
                acc = psum.tile([P, BANK], F32, name="acc")
                nc.tensor.matmul_mx(
                    out=acc[:, 0:n],
                    lhsT=w4_q[:, 2 * t * P : 2 * (t + 1) * P].bitcast(FP4X4),
                    lhsT_scale=w4_s[:, t * P : (t + 1) * P],
                    rhs=x_q[:].bitcast(FP8X4),
                    rhs_scale=x_s[:],
                    start=True,
                    stop=True,
                )
                accs[c, t] = acc

        def leave_psum(c, y):
            n = CHUNKS[c][1] - CHUNKS[c][0]
            ys[c] = y
            for t in range(PACK):
                nc.scalar.activation(y[:, t, :], accs[c, t][:, 0:n], ACT.Copy, scale=gain_sb[:, t : t + 1])

        def write(c):
            lo, hi = CHUNKS[c]
            for t in range(PACK):
                nc.vector.tensor_tensor(
                    pages[t][:].indirect(entries(list4, lo, hi)), ys[c][:, t, :], wgo_sb[:, t, lo:hi], MULT
                )
                if hi == PJ:
                    nc.sync.dma_start(out=out_rows[t], in_=pages[t][:])

        widths = [hi - lo for lo, hi in CHUNKS]
        fetch(0, held("x0", [P, PACK, widths[0]], F32))
        fetch(1, held("x1", [P, PACK, widths[1]], F32))
        product(0, relay([P, PACK * widths[0]], BF16))
        fetch(2, relay([P, PACK, widths[2]], F32))
        leave_psum(0, held("y0", [P, PACK, widths[0]], F32))
        product(1, held("x_bf1", [P, PACK * widths[1]], BF16))
        product(2, held("x_bf2", [P, PACK * widths[2]], BF16))
        write(0)
        leave_psum(1, relay([P, PACK, widths[1]], F32))
        write(1)
        leave_psum(2, held("y2", [P, PACK, widths[2]], F32))
        write(2)
